import numpy as np
import ml_dtypes


def mxq(x, axis, fmt="e4m3"):
    dtype, down = {"e4m3": (ml_dtypes.float8_e4m3fn, 7), "e5m2": (ml_dtypes.float8_e5m2, 14)}[fmt]
    v = np.moveaxis(np.asarray(x, np.float32).astype(ml_dtypes.bfloat16).astype(np.float64), axis, -1)
    blocks = v.reshape(v.shape[:-1] + (-1, 32))
    amax = np.abs(blocks).max(-1, keepdims=True)
    byte = np.maximum(np.where(amax > 0, np.frexp(amax)[1] - 1 + 127, 0) - down, 1)
    scale = np.exp2(byte - 127.0)
    codes = (blocks / scale).astype(np.float32).astype(dtype).astype(np.float64)
    return np.moveaxis((codes * scale).reshape(v.shape), -1, axis)


WIDE = False


def mx_kscale(k):
    if not WIDE:
        return np.ones(k)
    levels = np.array([10, -10, 5, -5, 0])
    if k % 512:
        return np.exp2(np.random.permutation(np.resize(levels, k // 32))).repeat(32)
    a = np.empty((k // 512, 16))
    for p in range(k // 512):
        a[p, :8] = np.random.permutation(np.resize(levels, 8))
        for g in range(8):
            far = levels[np.abs(levels - a[p, g]) >= 10]
            a[p, g + 8] = far[np.random.randint(len(far))]
    return np.exp2(a.ravel()).repeat(32)


def f64(x):
    return np.asarray(x).astype(np.float64)


def striped(idx):
    return np.tile(idx.reshape(-1, 16).T, (8, 1)).astype(np.uint16)


def unstriped(offs):
    return offs[:16].T.reshape(-1).astype(np.int64)


K, T, E, C, N = 512, 1024, 2, 256, 256


def by_expert(wq, xq):
    return np.concatenate([wq[e].T @ xq[:, e * C:(e + 1) * C] for e in range(E)], axis=1)


def setup_inputs():
    n = np.random.standard_normal
    s = mx_kscale(K)[:, None]
    return {
        "xT": (n((K, T)) * s).astype(np.float32),
        "w": (n((E, K, N)) / np.sqrt(K) / s[None]).astype(np.float32),
        "offs": striped(np.random.permutation(T)[:E * C]),
    }


def reference(xT, w, offs):
    idx = unstriped(offs)
    xq = mxq(f64(xT)[:, idx], 0, "e4m3")
    y = by_expert(mxq(f64(w), 1, "e4m3"), xq)
    out = np.zeros((N, T))
    out[:, idx] = y
    return out

@@ -1,0 +1,134 @@
+from contextlib import ExitStack
+
+import concourse.mybir as mybir
+
+K, T, E, C, N = 512, 1024, 2, 256, 256
+FLOPS = 2 * K * N * E * C
+
+F32 = mybir.dt.float32
+BF16 = mybir.dt.bfloat16
+U32 = mybir.dt.uint32
+U16 = mybir.dt.uint16
+U8 = mybir.dt.uint8
+FP8X4 = mybir.dt.float8_e4m3fn_x4
+COPY = mybir.ActivationFunctionType.Copy
+
+P = 128
+PACK = 4
+SLOTS = E * C
+NB = N // P
+COLS = C // 16
+
+
+def tile_routed_moe_kernel(tc, xT, w, offs, out):
+    nc = tc.nc
+    with ExitStack() as ctx:
+        held = ctx.enter_context(tc.tile_pool(name="held", bufs=1))
+        psum = ctx.enter_context(tc.psum_pool(name="psum", bufs=1))
+
+        offsets = held.tile([P, SLOTS // 16], U16, name="offsets")
+        nc.sync.dma_start(offsets[:], offs)
+
+        x_view = xT.rearrange("(p t) n -> p t n", t=PACK)
+        planes = []
+        for t in range(PACK):
+            plane = held.tile([P, T], F32, name="plane%d" % t)
+            nc.sync.dma_start(plane[:], x_view[:, t, :])
+            planes.append(plane)
+
+        w_raw = []
+        for e in range(E):
+            raw = held.tile([P, PACK, N], F32, name="w_raw%d" % e)
+            nc.sync.dma_start(raw[:], w[e].rearrange("(p j) n -> p j n", j=PACK))
+            w_raw.append(raw)
+
+        windows = []
+        for b in range(NB):
+            window = held.tile([P, T], F32, name="window%d" % b)
+            nc.vector.memset(window[:], 0.0)
+            windows.append(window)
+
+        def expert_offsets(e):
+            return offsets[:, e * COLS : (e + 1) * COLS]
+
+        x_grouped = held.tile([P, SLOTS, PACK], BF16, name="x_grouped", align_bytes=64)
+        x_codes = held.tile([P, SLOTS], U32, name="x_codes", align_bytes=64)
+        x_scales = held.tile([P, SLOTS], U8, name="x_scales", align_bytes=64)
+        w_grouped, w_codes, w_scales = [], [], []
+        for e in range(E):
+            w_grouped.append(held.tile([P, N, PACK], BF16, name="w_grouped%d" % e, align_bytes=64))
+            w_codes.append(held.tile([P, N], U32, name="w_codes%d" % e, align_bytes=64))
+            w_scales.append(held.tile([P, N], U8, name="w_scales%d" % e, align_bytes=64))
+
+        rounded = []
+        for t in range(2):
+            plane16 = held.tile([P, T], BF16, name="plane16_%d" % t)
+            nc.vector.tensor_copy(out=plane16[:], in_=planes[t][:])
+            rounded.append(plane16)
+
+        def scalar_gather(t):
+            nc.scalar.activation(
+                out=x_grouped[:, :, t], in_=rounded[t][:].indirect(offsets[:]), func=COPY
+            )
+
+        def interleave_w(engine_copy, e, lo, hi):
+            engine_copy(
+                out=w_grouped[e][:, lo:hi, :].rearrange("p (c i) j -> p c j i", i=4),
+                in_=w_raw[e][:, :, lo:hi].rearrange("p j (c i) -> p c j i", i=4),
+            )
+
+        def quantize_x(e):
+            nc.vector.quantize_mx(
+                out=x_codes[:, e * C : (e + 1) * C].bitcast(FP8X4),
+                scales=x_scales[:, e * C : (e + 1) * C],
+                in_=x_grouped[:, e * C : (e + 1) * C, :].rearrange("p n j -> p (n j)"),
+            )
+
+        def quantize_w(e, lo, hi):
+            nc.vector.quantize_mx(
+                out=w_codes[e][:, lo:hi].bitcast(FP8X4),
+                scales=w_scales[e][:, lo:hi],
+                in_=w_grouped[e][:, lo:hi, :].rearrange("p n j -> p (n j)"),
+            )
+
+        def multiply(e, b):
+            acc = psum.tile([P, C], F32, name="acc%d_%d" % (e, b))
+            nc.tensor.matmul_mx(
+                out=acc[:],
+                lhsT=w_codes[e][:, b * P : (b + 1) * P].bitcast(FP8X4),
+                lhsT_scale=w_scales[e][:, b * P : (b + 1) * P],
+                rhs=x_codes[:, e * C : (e + 1) * C].bitcast(FP8X4),
+                rhs_scale=x_scales[:, e * C : (e + 1) * C],
+                start=True,
+                stop=True,
+            )
+            sums = held.tile([P, C], F32, name="sums%d_%d" % (e, b))
+            nc.scalar.copy(out=sums[:], in_=acc[:])
+            return sums
+
+        def scatter(b, e, sums):
+            nc.vector.tensor_copy(windows[b][:].indirect(expert_offsets(e)), sums[:])
+
+        scalar_gather(0)
+        scalar_gather(1)
+        nc.vector.tensor_copy(x_grouped[:, :, 2], planes[2][:].indirect(offsets[:]))
+        nc.vector.tensor_copy(x_grouped[:, 0:C, 3], planes[3][:].indirect(expert_offsets(0)))
+        interleave_w(nc.scalar.copy, 0, 0, P)
+        interleave_w(nc.scalar.copy, 0, P, N)
+        quantize_x(0)
+        quantize_w(0, 0, P)
+        sums00 = multiply(0, 0)
+        nc.vector.tensor_copy(x_grouped[:, C:SLOTS, 3], planes[3][:].indirect(expert_offsets(1)))
+        quantize_x(1)
+        quantize_w(0, P, N)
+        sums01 = multiply(0, 1)
+        scatter(0, 0, sums00)
+        interleave_w(nc.scalar.copy, 1, 0, N)
+        quantize_w(1, 0, N)
+        sums10 = multiply(1, 0)
+        sums11 = multiply(1, 1)
+        scatter(1, 0, sums01)
+        scatter(0, 1, sums10)
+        nc.sync.dma_start(out[0:P, :], windows[0][:])
+        scatter(1, 1, sums11)
+        nc.sync.dma_start(out[P : 2 * P, :], windows[1][:])

@@ -27,7 +27,6 @@ def tile_routed_moe_kernel(tc, xT, w, offs, out):
         psum = ctx.enter_context(tc.psum_pool(name="psum", bufs=1))
 
         offsets = held.tile([P, SLOTS // 16], U16, name="offsets")
-        nc.sync.dma_start(offsets[:], offs)
 
         x_view = xT.rearrange("(p t) n -> p t n", t=PACK)
         planes = []
@@ -35,6 +34,8 @@ def tile_routed_moe_kernel(tc, xT, w, offs, out):
             plane = held.tile([P, T], F32, name="plane%d" % t)
             nc.sync.dma_start(plane[:], x_view[:, t, :])
             planes.append(plane)
+            if t == 0:
+                nc.sync.dma_start(offsets[:], offs)
 
         w_raw = []
         for e in range(E):

@@ -28,6 +28,11 @@ def tile_routed_moe_kernel(tc, xT, w, offs, out):
 
         offsets = held.tile([P, SLOTS // 16], U16, name="offsets")
 
+        warm_in = held.tile([P, 1], F32, name="warm_in")
+        warm_out = held.tile([P, 1], F32, name="warm_out")
+        nc.gpsimd.memset(warm_in[:], 0.0)
+        nc.scalar.activation(out=warm_out[:], in_=warm_in[:], func=COPY)
+
         x_view = xT.rearrange("(p t) n -> p t n", t=PACK)
         planes = []
         for t in range(PACK):

@@ -18,6 +18,7 @@ PACK = 4
 SLOTS = E * C
 NB = N // P
 COLS = C // 16
+SCALAR_SLOTS = 384
 
 
 def tile_routed_moe_kernel(tc, xT, w, offs, out):
@@ -42,11 +43,11 @@ def tile_routed_moe_kernel(tc, xT, w, offs, out):
             if t == 0:
                 nc.sync.dma_start(offsets[:], offs)
 
-        w_raw = []
-        for e in range(E):
-            raw = held.tile([P, PACK, N], F32, name="w_raw%d" % e)
-            nc.sync.dma_start(raw[:], w[e].rearrange("(p j) n -> p j n", j=PACK))
-            w_raw.append(raw)
+        w_raw = {}
+        for e, lo, hi in ((0, 0, P), (0, P, N), (1, 0, N)):
+            raw = held.tile([P, PACK, hi - lo], F32, name="w_raw%d_%d" % (e, lo))
+            nc.sync.dma_start(raw[:], w[e].rearrange("(p j) n -> p j n", j=PACK)[:, :, lo:hi])
+            w_raw[(e, lo)] = raw
 
         windows = []
         for b in range(NB):
@@ -58,11 +59,15 @@ def tile_routed_moe_kernel(tc, xT, w, offs, out):
             return offsets[:, e * COLS : (e + 1) * COLS]
 
         x_grouped = held.tile([P, SLOTS, PACK], BF16, name="x_grouped", align_bytes=64)
-        x_codes = held.tile([P, SLOTS], U32, name="x_codes", align_bytes=64)
+        x_codes = {0: held.tile([P, C], U32, name="x_codes0", align_bytes=64)}
         x_scales = held.tile([P, SLOTS], U8, name="x_scales", align_bytes=64)
-        w_grouped, w_codes, w_scales = [], [], []
+        w_grouped = {
+            (0, 0): held.tile([P, P, PACK], BF16, name="w_grouped0_0", tag="handed_on", align_bytes=64),
+            (0, P): held.tile([P, P, PACK], BF16, name="w_grouped0_128", align_bytes=64),
+            (1, 0): held.tile([P, N, PACK], BF16, name="w_grouped1_0", align_bytes=64),
+        }
+        w_codes, w_scales = [], []
         for e in range(E):
-            w_grouped.append(held.tile([P, N, PACK], BF16, name="w_grouped%d" % e, align_bytes=64))
             w_codes.append(held.tile([P, N], U32, name="w_codes%d" % e, align_bytes=64))
             w_scales.append(held.tile([P, N], U8, name="w_scales%d" % e, align_bytes=64))
 
@@ -71,21 +76,27 @@ def tile_routed_moe_kernel(tc, xT, w, offs, out):
             plane16 = held.tile([P, T], BF16, name="plane16_%d" % t)
             nc.vector.tensor_copy(out=plane16[:], in_=planes[t][:])
             rounded.append(plane16)
+            nc.vector.tensor_copy(
+                x_grouped[:, SCALAR_SLOTS:SLOTS, t],
+                planes[t][:].indirect(offsets[:, SCALAR_SLOTS // 16 : SLOTS // 16]),
+            )
 
         def scalar_gather(t):
             nc.scalar.activation(
-                out=x_grouped[:, :, t], in_=rounded[t][:].indirect(offsets[:]), func=COPY
+                out=x_grouped[:, 0:SCALAR_SLOTS, t],
+                in_=rounded[t][:].indirect(offsets[:, 0 : SCALAR_SLOTS // 16]),
+                func=COPY,
             )
 
         def interleave_w(engine_copy, e, lo, hi):
             engine_copy(
-                out=w_grouped[e][:, lo:hi, :].rearrange("p (c i) j -> p c j i", i=4),
-                in_=w_raw[e][:, :, lo:hi].rearrange("p j (c i) -> p c j i", i=4),
+                out=w_grouped[(e, lo)][:].rearrange("p (c i) j -> p c j i", i=4),
+                in_=w_raw[(e, lo)][:].rearrange("p j (c i) -> p c j i", i=4),
             )
 
         def quantize_x(e):
             nc.vector.quantize_mx(
-                out=x_codes[:, e * C : (e + 1) * C].bitcast(FP8X4),
+                out=x_codes[e][:].bitcast(FP8X4),
                 scales=x_scales[:, e * C : (e + 1) * C],
                 in_=x_grouped[:, e * C : (e + 1) * C, :].rearrange("p n j -> p (n j)"),
             )
@@ -94,7 +105,7 @@ def tile_routed_moe_kernel(tc, xT, w, offs, out):
             nc.vector.quantize_mx(
                 out=w_codes[e][:, lo:hi].bitcast(FP8X4),
                 scales=w_scales[e][:, lo:hi],
-                in_=w_grouped[e][:, lo:hi, :].rearrange("p n j -> p (n j)"),
+                in_=w_grouped[(e, lo)][:].rearrange("p n j -> p (n j)"),
             )
 
         def multiply(e, b):
@@ -103,7 +114,7 @@ def tile_routed_moe_kernel(tc, xT, w, offs, out):
                 out=acc[:],
                 lhsT=w_codes[e][:, b * P : (b + 1) * P].bitcast(FP8X4),
                 lhsT_scale=w_scales[e][:, b * P : (b + 1) * P],
-                rhs=x_codes[:, e * C : (e + 1) * C].bitcast(FP8X4),
+                rhs=x_codes[e][:].bitcast(FP8X4),
                 rhs_scale=x_scales[:, e * C : (e + 1) * C],
                 start=True,
                 stop=True,
@@ -124,6 +135,7 @@ def tile_routed_moe_kernel(tc, xT, w, offs, out):
         quantize_x(0)
         quantize_w(0, 0, P)
         sums00 = multiply(0, 0)
+        x_codes[1] = held.tile([P, C], U32, name="x_codes1", tag="handed_on", align_bytes=64)
         nc.vector.tensor_copy(x_grouped[:, C:SLOTS, 3], planes[3][:].indirect(expert_offsets(1)))
         quantize_x(1)
         quantize_w(0, P, N)

@@ -132,8 +132,8 @@ def tile_routed_moe_kernel(tc, xT, w, offs, out):
         nc.vector.tensor_copy(x_grouped[:, 0:C, 3], planes[3][:].indirect(expert_offsets(0)))
         interleave_w(nc.scalar.copy, 0, 0, P)
         interleave_w(nc.scalar.copy, 0, P, N)
-        quantize_x(0)
         quantize_w(0, 0, P)
+        quantize_x(0)
         sums00 = multiply(0, 0)
         x_codes[1] = held.tile([P, C], U32, name="x_codes1", tag="handed_on", align_bytes=64)
         nc.vector.tensor_copy(x_grouped[:, C:SLOTS, 3], planes[3][:].indirect(expert_offsets(1)))

from contextlib import ExitStack

import concourse.mybir as mybir

K, T, E, C, N = 512, 1024, 2, 256, 256
FLOPS = 2 * K * N * E * C

F32 = mybir.dt.float32
BF16 = mybir.dt.bfloat16
U32 = mybir.dt.uint32
U16 = mybir.dt.uint16
U8 = mybir.dt.uint8
FP8X4 = mybir.dt.float8_e4m3fn_x4
COPY = mybir.ActivationFunctionType.Copy

P = 128
PACK = 4
SLOTS = E * C
NB = N // P
COLS = C // 16
SCALAR_SLOTS = 384


def tile_routed_moe_kernel(tc, xT, w, offs, out):
    nc = tc.nc
    with ExitStack() as ctx:
        held = ctx.enter_context(tc.tile_pool(name="held", bufs=1))
        psum = ctx.enter_context(tc.psum_pool(name="psum", bufs=1))

        offsets = held.tile([P, SLOTS // 16], U16, name="offsets")

        warm_in = held.tile([P, 1], F32, name="warm_in")
        warm_out = held.tile([P, 1], F32, name="warm_out")
        nc.gpsimd.memset(warm_in[:], 0.0)
        nc.scalar.activation(out=warm_out[:], in_=warm_in[:], func=COPY)

        x_view = xT.rearrange("(p t) n -> p t n", t=PACK)
        planes = []
        for t in range(PACK):
            plane = held.tile([P, T], F32, name="plane%d" % t)
            nc.sync.dma_start(plane[:], x_view[:, t, :])
            planes.append(plane)
            if t == 0:
                nc.sync.dma_start(offsets[:], offs)

        w_raw = {}
        for e, lo, hi in ((0, 0, P), (0, P, N), (1, 0, N)):
            raw = held.tile([P, PACK, hi - lo], F32, name="w_raw%d_%d" % (e, lo))
            nc.sync.dma_start(raw[:], w[e].rearrange("(p j) n -> p j n", j=PACK)[:, :, lo:hi])
            w_raw[(e, lo)] = raw

        windows = []
        for b in range(NB):
            window = held.tile([P, T], F32, name="window%d" % b)
            nc.vector.memset(window[:], 0.0)
            windows.append(window)

        def expert_offsets(e):
            return offsets[:, e * COLS : (e + 1) * COLS]

        x_grouped = held.tile([P, SLOTS, PACK], BF16, name="x_grouped", align_bytes=64)
        x_codes = {0: held.tile([P, C], U32, name="x_codes0", align_bytes=64)}
        x_scales = held.tile([P, SLOTS], U8, name="x_scales", align_bytes=64)
        w_grouped = {
            (0, 0): held.tile([P, P, PACK], BF16, name="w_grouped0_0", tag="handed_on", align_bytes=64),
            (0, P): held.tile([P, P, PACK], BF16, name="w_grouped0_128", align_bytes=64),
            (1, 0): held.tile([P, N, PACK], BF16, name="w_grouped1_0", align_bytes=64),
        }
        w_codes, w_scales = [], []
        for e in range(E):
            w_codes.append(held.tile([P, N], U32, name="w_codes%d" % e, align_bytes=64))
            w_scales.append(held.tile([P, N], U8, name="w_scales%d" % e, align_bytes=64))

        rounded = []
        for t in range(2):
            plane16 = held.tile([P, T], BF16, name="plane16_%d" % t)
            nc.vector.tensor_copy(out=plane16[:], in_=planes[t][:])
            rounded.append(plane16)
            nc.vector.tensor_copy(
                x_grouped[:, SCALAR_SLOTS:SLOTS, t],
                planes[t][:].indirect(offsets[:, SCALAR_SLOTS // 16 : SLOTS // 16]),
            )

        def scalar_gather(t):
            nc.scalar.activation(
                out=x_grouped[:, 0:SCALAR_SLOTS, t],
                in_=rounded[t][:].indirect(offsets[:, 0 : SCALAR_SLOTS // 16]),
                func=COPY,
            )

        def interleave_w(engine_copy, e, lo, hi):
            engine_copy(
                out=w_grouped[(e, lo)][:].rearrange("p (c i) j -> p c j i", i=4),
                in_=w_raw[(e, lo)][:].rearrange("p j (c i) -> p c j i", i=4),
            )

        def quantize_x(e):
            nc.vector.quantize_mx(
                out=x_codes[e][:].bitcast(FP8X4),
                scales=x_scales[:, e * C : (e + 1) * C],
                in_=x_grouped[:, e * C : (e + 1) * C, :].rearrange("p n j -> p (n j)"),
            )

        def quantize_w(e, lo, hi):
            nc.vector.quantize_mx(
                out=w_codes[e][:, lo:hi].bitcast(FP8X4),
                scales=w_scales[e][:, lo:hi],
                in_=w_grouped[(e, lo)][:].rearrange("p n j -> p (n j)"),
            )

        def multiply(e, b):
            acc = psum.tile([P, C], F32, name="acc%d_%d" % (e, b))
            nc.tensor.matmul_mx(
                out=acc[:],
                lhsT=w_codes[e][:, b * P : (b + 1) * P].bitcast(FP8X4),
                lhsT_scale=w_scales[e][:, b * P : (b + 1) * P],
                rhs=x_codes[e][:].bitcast(FP8X4),
                rhs_scale=x_scales[:, e * C : (e + 1) * C],
                start=True,
                stop=True,
            )
            sums = held.tile([P, C], F32, name="sums%d_%d" % (e, b))
            nc.scalar.copy(out=sums[:], in_=acc[:])
            return sums

        def scatter(b, e, sums):
            nc.vector.tensor_copy(windows[b][:].indirect(expert_offsets(e)), sums[:])

        scalar_gather(0)
        scalar_gather(1)
        nc.vector.tensor_copy(x_grouped[:, :, 2], planes[2][:].indirect(offsets[:]))
        nc.vector.tensor_copy(x_grouped[:, 0:C, 3], planes[3][:].indirect(expert_offsets(0)))
        interleave_w(nc.scalar.copy, 0, 0, P)
        interleave_w(nc.scalar.copy, 0, P, N)
        quantize_w(0, 0, P)
        quantize_x(0)
        sums00 = multiply(0, 0)
        x_codes[1] = held.tile([P, C], U32, name="x_codes1", tag="handed_on", align_bytes=64)
        nc.vector.tensor_copy(x_grouped[:, C:SLOTS, 3], planes[3][:].indirect(expert_offsets(1)))
        quantize_x(1)
        quantize_w(0, P, N)
        sums01 = multiply(0, 1)
        scatter(0, 0, sums00)
        interleave_w(nc.scalar.copy, 1, 0, N)
        quantize_w(1, 0, N)
        sums10 = multiply(1, 0)
        sums11 = multiply(1, 1)
        scatter(1, 0, sums01)
        scatter(0, 1, sums10)
        nc.sync.dma_start(out[0:P, :], windows[0][:])
        scatter(1, 1, sums11)
        nc.sync.dma_start(out[P : 2 * P, :], windows[1][:])
